import numpy as np
import ml_dtypes


def mxq(x, axis, fmt="e4m3"):
    dtype, down = {"e4m3": (ml_dtypes.float8_e4m3fn, 7), "e5m2": (ml_dtypes.float8_e5m2, 14)}[fmt]
    v = np.moveaxis(np.asarray(x, np.float32).astype(ml_dtypes.bfloat16).astype(np.float64), axis, -1)
    blocks = v.reshape(v.shape[:-1] + (-1, 32))
    amax = np.abs(blocks).max(-1, keepdims=True)
    byte = np.maximum(np.where(amax > 0, np.frexp(amax)[1] - 1 + 127, 0) - down, 1)
    scale = np.exp2(byte - 127.0)
    codes = (blocks / scale).astype(np.float32).astype(dtype).astype(np.float64)
    return np.moveaxis((codes * scale).reshape(v.shape), -1, axis)


WIDE = False


def mx_kscale(k):
    if not WIDE:
        return np.ones(k)
    levels = np.array([10, -10, 5, -5, 0])
    if k % 512:
        return np.exp2(np.random.permutation(np.resize(levels, k // 32))).repeat(32)
    a = np.empty((k // 512, 16))
    for p in range(k // 512):
        a[p, :8] = np.random.permutation(np.resize(levels, 8))
        for g in range(8):
            far = levels[np.abs(levels - a[p, g]) >= 10]
            a[p, g + 8] = far[np.random.randint(len(far))]
    return np.exp2(a.ravel()).repeat(32)


def f64(x):
    return np.asarray(x).astype(np.float64)


def striped(idx):
    return np.tile(idx.reshape(-1, 16).T, (8, 1)).astype(np.uint16)


def unstriped(offs):
    return offs[:16].T.reshape(-1).astype(np.int64)


def striped8(idx):
    return np.concatenate([x.reshape(-1, 16).T for x in idx]).astype(np.uint16)


def runs(offs, k):
    lists = np.stack([offs[16 * r : 16 * r + 16].T.reshape(-1) for r in range(8)]).astype(np.int64)
    return lists[np.arange(k) % 512 // 64]


def pack_weight(w):
    k, n = w.shape
    w = f64(np.asarray(w, np.float32).astype(ml_dtypes.bfloat16)).reshape(k // 32, 32, n)
    amax = np.abs(w).max(1)
    byte = np.clip(np.where(amax > 0, np.frexp(amax)[1] - 1 + 127 - 7, 1), 1, 254)
    scaled = (w * np.exp2(127.0 - byte)[:, None, :]).reshape(k, n).astype(np.float32)
    words = np.ascontiguousarray(scaled.reshape(k // 512, 128, 4, n).transpose(0, 1, 3, 2)).astype(ml_dtypes.float8_e4m3fn).view(np.uint8)
    return words, np.ascontiguousarray(byte.astype(np.uint8).reshape(k // 512, 16, n))


def unpack_weight(words, scales):
    g, p, n, _ = words.shape
    vals = np.ascontiguousarray(words).view(ml_dtypes.float8_e4m3fn).astype(np.float64) * np.repeat(np.exp2(scales.astype(np.float64) - 127.0), 8, axis=1)[..., None]
    return vals.transpose(0, 1, 3, 2).reshape(g * 512, n)


def sigmoid(v):
    return 1.0 / (1.0 + np.exp(-np.maximum(v, -700.0)))

def planes(y):
    n, m = y.shape
    v = y.astype(np.float32).astype(ml_dtypes.bfloat16).astype(np.float64).reshape(n // 32, 32, m)
    top = np.abs(v).max(1)
    byte = np.clip(np.where(top > 0, np.frexp(top)[1] - 1 + 127 - 7, 1), 1, 254)
    codes = (v * np.exp2(127.0 - byte)[:, None, :]).reshape(n, m).astype(np.float32).astype(ml_dtypes.float8_e4m3fn).view(np.uint8)
    words = codes.reshape(n // 512, 128, 4, m).transpose(0, 1, 3, 2)
    return np.ascontiguousarray(words), np.ascontiguousarray(byte.astype(np.uint8).reshape(n // 512, 16, m))


K, T, S, N, H, U = 512, 2048, 512, 512, 512, 1024


def setup_inputs():
    n = np.random.standard_normal
    s = mx_kscale(K)[:, None]
    u = mx_kscale(H)
    packed_xT = pack_weight(n((K, T)) * s)
    packed_w1 = pack_weight(n((K, H)) / np.sqrt(K) / s)
    packed_w2 = pack_weight(n((H, N)) / np.sqrt(H) / u[:, None])
    return {
        "x_words": packed_xT[0],
        "x_scales": packed_xT[1],
        "w1_words": packed_w1[0],
        "w1_scales": packed_w1[1],
        "gn": (np.random.uniform(0.5, 1.5, (H, 1)) * u[:, None]).astype(np.float32),
        "w2_words": packed_w2[0],
        "w2_scales": packed_w2[1],
        "mem": n((N, U)).astype(np.float32),
        "offs": striped(np.random.permutation(T)[:S]),
        "c1": striped8(np.stack([np.random.permutation(S) for _ in range(8)])),
        "c2": striped8(np.stack([np.random.permutation(S) for _ in range(8)])),
        "c3": striped8(np.stack([np.random.permutation(S) for _ in range(8)])),
        "slot": striped8(np.stack([np.random.permutation(U)[:S] for _ in range(8)])),
    }


def reference(x_words, x_scales, w1_words, w1_scales, gn, w2_words, w2_scales, mem, offs, c1, c2, c3, slot):
    xq = unpack_weight(x_words, x_scales)[:, unstriped(offs)]
    p = sigmoid(unpack_weight(w1_words, w1_scales).T @ xq)
    a = p[np.arange(H)[:, None], runs(c1, H)]
    b = p[np.arange(H)[:, None], runs(c2, H)]
    c = p[np.arange(H)[:, None], runs(c3, H)]
    z = f64(gn) * ((-1.0 * a + 1) * (-1.0 * b + 1) - (a * c))
    h = unpack_weight(w2_words, w2_scales).T @ mxq(z, 0, "e4m3")
    out = f64(mem).copy()
    out[np.arange(N)[:, None], runs(slot, N)] = h
    return (out,) + planes(out)

@@ -1,0 +1,212 @@
+from contextlib import ExitStack
+
+import concourse.mybir as mybir
+
+K, T, S, N, H, U = 512, 2048, 512, 512, 512, 1024
+FLOPS = 2 * K * H * S + 2 * H * N * S
+
+F32 = mybir.dt.float32
+BF16 = mybir.dt.bfloat16
+I32 = mybir.dt.int32
+U32 = mybir.dt.uint32
+U16 = mybir.dt.uint16
+U8 = mybir.dt.uint8
+FP8X4 = mybir.dt.float8_e4m3fn_x4
+ACT = mybir.ActivationFunctionType
+ALU = mybir.AluOpType
+
+P = 128
+PACK = 4
+CHUNK = 128
+SPLIT = 512
+
+
+def load_scale_rows(queue, plane, rows):
+    for q in range(4):
+        queue.dma_start(plane[32 * q : 32 * q + 4, :].bitcast(I32), rows[4 * q : 4 * q + 4, :].bitcast(I32))
+
+
+def tile_picked_noisygate_none_po_kernel(
+    tc, x_words, x_scales, w1_words, w1_scales, gn, w2_words, w2_scales, mem, offs, c1, c2, c3, slot, out_0, out_1, out_2
+):
+    nc = tc.nc
+    with ExitStack() as ctx:
+        lists = ctx.enter_context(tc.tile_pool(name="lists", bufs=1))
+        keep = ctx.enter_context(tc.tile_pool(name="keep", bufs=1))
+        work = ctx.enter_context(tc.tile_pool(name="work", bufs=2))
+        once = ctx.enter_context(tc.tile_pool(name="once", bufs=1))
+        psum = ctx.enter_context(tc.psum_pool(name="psum", bufs=1))
+        psum2 = ctx.enter_context(tc.psum_pool(name="psum2", bufs=2))
+
+        offs_sb = lists.tile([P, S // 16], U16, name="offs_sb")
+        c1_sb = lists.tile([P, S // 16], U16, name="c1_sb")
+        c2_sb = lists.tile([P, S // 16], U16, name="c2_sb")
+        c3_sb = lists.tile([P, S // 16], U16, name="c3_sb")
+        slot_sb = lists.tile([P, S // 16], U16, name="slot_sb")
+
+        xs = keep.tile([P, T], U8, name="xs", align_bytes=64)
+        xw = keep.tile([P, T], I32, name="xw", align_bytes=64)
+        w1w = keep.tile([P, H], I32, name="w1w", align_bytes=64)
+        w1s = keep.tile([P, H], U8, name="w1s", align_bytes=64)
+        w2w = keep.tile([P, N], I32, name="w2w", align_bytes=64)
+        w2s = keep.tile([P, N], U8, name="w2s", align_bytes=64)
+        gain = keep.tile([P, PACK], F32, name="gain")
+        warm = keep.tile([P, 1], F32, name="warm")
+        warm2 = keep.tile([P, 1], F32, name="warm2")
+
+        nc.vector.memset(xs[:].bitcast(I32), 0)
+        nc.vector.memset(w1s[:].bitcast(I32), 0)
+        nc.vector.memset(w2s[:].bitcast(I32), 0)
+        nc.gpsimd.memset(warm[:], 0.0)
+        nc.scalar.activation(warm2[:], warm[:], ACT.Sigmoid)
+
+        load_scale_rows(nc.sync, xs, x_scales[0])
+        nc.sync.dma_start(offs_sb[:], offs)
+        nc.sync.dma_start(w1w[:], w1_words[0].rearrange("p n t -> p (n t)").bitcast(I32))
+        nc.sync.dma_start(xw[:], x_words[0].rearrange("p n t -> p (n t)").bitcast(I32))
+        load_scale_rows(nc.sync, w1s, w1_scales[0])
+        nc.sync.dma_start(c2_sb[:], c2)
+        nc.sync.dma_start(c3_sb[:], c3)
+        nc.sync.dma_start(c1_sb[:], c1)
+        nc.sync.dma_start(gain[:], gn.rearrange("(p t) o -> p (t o)", t=PACK))
+        nc.sync.dma_start(w2w[:], w2_words[0].rearrange("p n t -> p (n t)").bitcast(I32))
+        load_scale_rows(nc.sync, w2s, w2_scales[0])
+        nc.sync.dma_start(slot_sb[:], slot)
+        page = [keep.tile([P, U], F32, name="page%d" % t) for t in range(PACK)]
+        mem_rows = mem.rearrange("(p t) u -> p t u", t=PACK)
+        for t in range(PACK):
+            nc.sync.dma_start(page[t][:], mem_rows[:, t, :])
+
+        xs_g = keep.tile([P, S], U8, name="xs_g", align_bytes=64)
+        xw_g = keep.tile([P, S], U32, name="xw_g", align_bytes=64)
+        nc.vector.tensor_copy(xs_g[:], xs[:].indirect(offs_sb[:]))
+        w1w_d = keep.tile([P, H], I32, name="w1w_d", align_bytes=64)
+        w1s_d = keep.tile([P, H], U8, name="w1s_d", align_bytes=64)
+        nc.vector.tensor_copy(w1w_d[:].rearrange("p (t m) -> p t m", t=PACK), w1w[:].rearrange("p (m t) -> p t m", t=PACK))
+        nc.vector.tensor_copy(xw_g[:], xw[:].bitcast(U32).indirect(offs_sb[:]))
+        nc.vector.tensor_copy(w1s_d[:].rearrange("p (t m) -> p t m", t=PACK), w1s[:].rearrange("p (m t) -> p t m", t=PACK))
+        w2w_d = keep.tile([P, N], I32, name="w2w_d", align_bytes=64)
+        w2s_d = keep.tile([P, N], U8, name="w2s_d", align_bytes=64)
+        nc.vector.tensor_copy(w2w_d[:].rearrange("p (t m) -> p t m", t=PACK), w2w[:].rearrange("p (m t) -> p t m", t=PACK))
+        nc.vector.tensor_copy(w2s_d[:].rearrange("p (t m) -> p t m", t=PACK), w2s[:].rearrange("p (m t) -> p t m", t=PACK))
+
+        pre = [keep.tile([P, S], F32, name="pre%d" % t) for t in range(PACK)]
+        for t in range(PACK):
+            cols = slice(P * t, P * (t + 1))
+            acc = psum.tile([P, S], F32, name="acc%d" % t)
+            nc.tensor.matmul_mx(
+                acc[:], lhsT=w1w_d[:, cols].bitcast(FP8X4), lhsT_scale=w1s_d[:, cols],
+                rhs=xw_g[:].bitcast(FP8X4), rhs_scale=xs_g[:], start=True, stop=True,
+            )
+            nc.vector.tensor_copy(pre[t][:], acc[:])
+
+        n = CHUNK
+        nch = S // n
+        picked = {}
+
+        def fetch(items, tag):
+            batch = once.tile([P, len(items), 3, n], F32, name="batch", tag=tag, align_bytes=64)
+            for i, (k, t) in enumerate(items):
+                lc = slice(k * n // 16, (k + 1) * n // 16)
+                nc.scalar.activation(batch[:, i, 0, :], pre[t][:].indirect(c1_sb[:, lc]), ACT.Sigmoid)
+                nc.scalar.activation(batch[:, i, 1, :], pre[t][:].indirect(c3_sb[:, lc]), ACT.Sigmoid)
+                nc.scalar.activation(batch[:, i, 2, :], pre[t][:].indirect(c2_sb[:, lc]), ACT.Sigmoid, scale=-1.0)
+                picked[(k, t)] = (batch, i)
+
+        terms = {}
+
+        def products(k, t):
+            if t == 0:
+                terms[k] = (
+                    work.tile([P, PACK, n], F32, name="na"),
+                    work.tile([P, PACK, n], F32, name="first"),
+                    once.tile([P, PACK, n], F32, name="second", tag="second%d" % (k % 2)),
+                )
+            na, first, second = terms[k]
+            batch, i = picked[(k, t)]
+            g = gain[:, t : t + 1]
+            nc.vector.tensor_scalar(na[:, t, :], batch[:, i, 0, :], -1.0, 1.0, ALU.mult, ALU.add)
+            nc.vector.scalar_tensor_tensor(second[:, t, :], batch[:, i, 0, :], g, batch[:, i, 1, :], ALU.mult, ALU.mult)
+            nc.vector.scalar_tensor_tensor(first[:, t, :], na[:, t, :], g, batch[:, i, 2, :], ALU.mult, ALU.mult)
+
+        def quantise(k):
+            na, first, second = terms[k]
+            z = work.tile([P, n, PACK], BF16, name="z", align_bytes=64)
+            nc.vector.tensor_tensor(
+                z[:].rearrange("p (c i) t -> p c t i", i=4),
+                first[:].rearrange("p t (c i) -> p c t i", i=4),
+                second[:].rearrange("p t (c i) -> p c t i", i=4),
+                ALU.subtract,
+            )
+            zw = once.tile([P, n], U32, name="zw", tag="turn%d" % (k % 2), align_bytes=64)
+            zs = work.tile([P, n], U8, name="zs", align_bytes=64)
+            nc.vector.quantize_mx(zw[:].bitcast(FP8X4), zs[:], z[:].rearrange("p n t -> p (n t)"))
+            return zw, zs
+
+        def multiply(zw, zs):
+            hacc = psum2.tile([P, PACK, n], F32, name="hacc")
+            for t in range(PACK):
+                cols = slice(P * t, P * (t + 1))
+                nc.tensor.matmul_mx(
+                    hacc[:, t, :], lhsT=w2w_d[:, cols].bitcast(FP8X4), lhsT_scale=w2s_d[:, cols],
+                    rhs=zw[:].bitcast(FP8X4), rhs_scale=zs[:], start=True, stop=True,
+                )
+            return hacc
+
+        def put(k, hacc, t0, t1, h):
+            lc = slice(k * n // 16, (k + 1) * n // 16)
+            nc.scalar.copy(h[:, 0 : t1 - t0, :], hacc[:, t0:t1, :])
+            for t in range(t0, t1):
+                nc.vector.tensor_copy(page[t][:].indirect(slot_sb[:, lc]), h[:, t - t0, :])
+
+        fetch([(0, 0), (0, 1), (0, 2)], "turn0")
+        fetch([(0, 3), (1, 0), (1, 1), (1, 2)], "turn1")
+        for t in range(PACK - 1):
+            products(0, t)
+        held = None
+        for k in range(nch):
+            products(k, PACK - 1)
+            zw, zs = quantise(k)
+            if k == nch - 1:
+                hb = once.tile([P, PACK, n], F32, name="hb", tag="second%d" % (k % 2))
+                put(k - 1, held, 2, PACK, hb)
+            hacc = multiply(zw, zs)
+            h = work.tile([P, PACK, n], F32, name="h")
+            if k == nch - 2:
+                put(k, hacc, 0, 2, h)
+                held = hacc
+            else:
+                put(k, hacc, 0, PACK, h)
+            if k + 1 < nch:
+                for t in range(PACK - 1):
+                    products(k + 1, t)
+                later = [(k + 1, PACK - 1)]
+                if k + 2 < nch:
+                    later = later + [(k + 2, t) for t in range(PACK - 1)]
+                fetch(later, "turn%d" % (k % 2))
+
+        out_rows = out_0.rearrange("(p t) u -> p t u", t=PACK)
+        y = keep.tile([P, PACK, U], BF16, name="y")
+        for t in range(PACK):
+            nc.sync.dma_start(out_rows[:, t, :], page[t][:])
+            if t < PACK - 1:
+                nc.scalar.copy(y[:, t, :], page[t][:])
+            else:
+                nc.vector.tensor_copy(y[:, t, :], page[t][:])
+        ow = keep.tile([P, U], I32, name="ow", align_bytes=64)
+        osc = keep.tile([P, U], U8, name="osc", align_bytes=64)
+        words_out = out_1[0].rearrange("p n t -> p (n t)").bitcast(I32)
+        for half in range(2):
+            cols = slice(half * SPLIT, (half + 1) * SPLIT)
+            yi = keep.tile([P, SPLIT, PACK], BF16, name="yi%d" % half, align_bytes=64)
+            dst = yi[:].rearrange("p (c i) t -> p c t i", i=4)
+            src = y[:, :, cols].rearrange("p t (c i) -> p c t i", i=4)
+            if half == 0:
+                nc.vector.tensor_copy(dst, src)
+            else:
+                nc.vector.tensor_copy(dst[:, 0:32], src[:, 0:32])
+                nc.scalar.copy(dst[:, 32:128], src[:, 32:128])
+            nc.vector.quantize_mx(ow[:, cols].bitcast(FP8X4), osc[:, cols], yi[:].rearrange("p n t -> p (n t)"))
+            nc.sync.dma_start(words_out[:, cols], ow[:, cols])
+        for q in range(4):
+            nc.sync.dma_start(out_2[0, 4 * q : 4 * q + 4, :].bitcast(I32), osc[32 * q : 32 * q + 4, :].bitcast(I32))

@@ -17,8 +17,9 @@ ALU = mybir.AluOpType
 
 P = 128
 PACK = 4
-CHUNK = 128
-SPLIT = 512
+CHUNK = 256
+AHEAD = 5
+SPLIT = 640
 
 
 def load_scale_rows(queue, plane, rows):
@@ -44,169 +45,184 @@ def tile_picked_noisygate_none_po_kernel(
         c3_sb = lists.tile([P, S // 16], U16, name="c3_sb")
         slot_sb = lists.tile([P, S // 16], U16, name="slot_sb")
 
-        xs = keep.tile([P, T], U8, name="xs", align_bytes=64)
-        xw = keep.tile([P, T], I32, name="xw", align_bytes=64)
-        w1w = keep.tile([P, H], I32, name="w1w", align_bytes=64)
-        w1s = keep.tile([P, H], U8, name="w1s", align_bytes=64)
+        xs = keep.tile([P, T], U8, name="xs", tag="reuse1", align_bytes=64)
+        xw = keep.tile([P, T], I32, name="xw", tag="reuse0", align_bytes=64)
+        w1w = keep.tile([P, H], I32, name="w1w", tag="reuse2", align_bytes=64)
+        w1s = keep.tile([P, H], U8, name="w1s", tag="reuse3", align_bytes=64)
         w2w = keep.tile([P, N], I32, name="w2w", align_bytes=64)
         w2s = keep.tile([P, N], U8, name="w2s", align_bytes=64)
         gain = keep.tile([P, PACK], F32, name="gain")
         warm = keep.tile([P, 1], F32, name="warm")
         warm2 = keep.tile([P, 1], F32, name="warm2")
 
-        nc.vector.memset(xs[:].bitcast(I32), 0)
+        nc.gpsimd.memset(xs[:].bitcast(I32), 0)
+        nc.gpsimd.memset(w2s[:].bitcast(I32), 0)
         nc.vector.memset(w1s[:].bitcast(I32), 0)
-        nc.vector.memset(w2s[:].bitcast(I32), 0)
-        nc.gpsimd.memset(warm[:], 0.0)
+        nc.vector.memset(warm[:], 0.0)
         nc.scalar.activation(warm2[:], warm[:], ACT.Sigmoid)
 
-        load_scale_rows(nc.sync, xs, x_scales[0])
         nc.sync.dma_start(offs_sb[:], offs)
         nc.sync.dma_start(w1w[:], w1_words[0].rearrange("p n t -> p (n t)").bitcast(I32))
+        nc.sync.dma_start(c2_sb[:], c2)
+        load_scale_rows(nc.sync, xs, x_scales[0])
         nc.sync.dma_start(xw[:], x_words[0].rearrange("p n t -> p (n t)").bitcast(I32))
         load_scale_rows(nc.sync, w1s, w1_scales[0])
-        nc.sync.dma_start(c2_sb[:], c2)
-        nc.sync.dma_start(c3_sb[:], c3)
-        nc.sync.dma_start(c1_sb[:], c1)
         nc.sync.dma_start(gain[:], gn.rearrange("(p t) o -> p (t o)", t=PACK))
+        nc.sync.dma_start(c1_sb[:], c1)
+        nc.sync.dma_start(c3_sb[:], c3)
         nc.sync.dma_start(w2w[:], w2_words[0].rearrange("p n t -> p (n t)").bitcast(I32))
         load_scale_rows(nc.sync, w2s, w2_scales[0])
         nc.sync.dma_start(slot_sb[:], slot)
-        page = [keep.tile([P, U], F32, name="page%d" % t) for t in range(PACK)]
-        mem_rows = mem.rearrange("(p t) u -> p t u", t=PACK)
-        for t in range(PACK):
-            nc.sync.dma_start(page[t][:], mem_rows[:, t, :])
 
         xs_g = keep.tile([P, S], U8, name="xs_g", align_bytes=64)
         xw_g = keep.tile([P, S], U32, name="xw_g", align_bytes=64)
         nc.vector.tensor_copy(xs_g[:], xs[:].indirect(offs_sb[:]))
-        w1w_d = keep.tile([P, H], I32, name="w1w_d", align_bytes=64)
-        w1s_d = keep.tile([P, H], U8, name="w1s_d", align_bytes=64)
-        nc.vector.tensor_copy(w1w_d[:].rearrange("p (t m) -> p t m", t=PACK), w1w[:].rearrange("p (m t) -> p t m", t=PACK))
         nc.vector.tensor_copy(xw_g[:], xw[:].bitcast(U32).indirect(offs_sb[:]))
-        nc.vector.tensor_copy(w1s_d[:].rearrange("p (t m) -> p t m", t=PACK), w1s[:].rearrange("p (m t) -> p t m", t=PACK))
-        w2w_d = keep.tile([P, N], I32, name="w2w_d", align_bytes=64)
-        w2s_d = keep.tile([P, N], U8, name="w2s_d", align_bytes=64)
-        nc.vector.tensor_copy(w2w_d[:].rearrange("p (t m) -> p t m", t=PACK), w2w[:].rearrange("p (m t) -> p t m", t=PACK))
-        nc.vector.tensor_copy(w2s_d[:].rearrange("p (t m) -> p t m", t=PACK), w2s[:].rearrange("p (m t) -> p t m", t=PACK))
 
-        pre = [keep.tile([P, S], F32, name="pre%d" % t) for t in range(PACK)]
+        def deal(raw, dtype, t0, t1, name):
+            dealt = keep.tile([P, t1 - t0, P], dtype, name=name, align_bytes=64)
+            nc.vector.tensor_copy(
+                dealt[:].rearrange("p t (c i) -> p c t i", i=4),
+                raw[:].rearrange("p (c i t) -> p c t i", i=4, t=PACK)[:, :, t0:t1, :],
+            )
+            return [dealt[:, t - t0, :] for t in range(t0, t1)]
+
+        w1w_d = deal(w1w, I32, 0, PACK, "w1w_d")
+        w1s_d = deal(w1s, U8, 0, 1, "w1s_head")
+        w1s_d = w1s_d + deal(w1s, U8, 1, PACK, "w1s_rest")
+        w2w_d = deal(w2w, I32, 0, PACK, "w2w_d")
+        w2s_d = deal(w2s, U8, 0, PACK, "w2s_d")
+
+        page = [keep.tile([P, U], F32, name="page%d" % t, tag="reuse%d" % t, align_bytes=64) for t in range(PACK)]
+        mem_rows = mem.rearrange("(p t) u -> p t u", t=PACK)
         for t in range(PACK):
-            cols = slice(P * t, P * (t + 1))
+            nc.sync.dma_start(page[t][:], mem_rows[:, t, :])
+
+        pre = {}
+        for t in range(PACK):
             acc = psum.tile([P, S], F32, name="acc%d" % t)
             nc.tensor.matmul_mx(
-                acc[:], lhsT=w1w_d[:, cols].bitcast(FP8X4), lhsT_scale=w1s_d[:, cols],
+                acc[:], lhsT=w1w_d[t].bitcast(FP8X4), lhsT_scale=w1s_d[t],
                 rhs=xw_g[:].bitcast(FP8X4), rhs_scale=xs_g[:], start=True, stop=True,
             )
-            nc.vector.tensor_copy(pre[t][:], acc[:])
-
+            pre[t] = keep.tile([P, S], F32, name="pre%d" % t)
+            if t == 0:
+                nc.scalar.activation(pre[t][:], acc[:], ACT.Sigmoid)
+            else:
+                nc.vector.tensor_copy(pre[t][:], acc[:])
         n = CHUNK
-        nch = S // n
+        first = [once.tile([P, PACK, n], F32, name="first%d" % k) for k in range(2)]
+        second = [once.tile([P, PACK, n], F32, name="second", tag="second%d" % k) for k in range(2)]
+
+        def entries(k):
+            return slice(k * n // 16, (k + 1) * n // 16)
+
+        gp = keep.tile([P, S], F32, name="gp")
+        gq = keep.tile([P, S], F32, name="gq")
+        nc.vector.tensor_scalar(gp[:], pre[0][:], gain[:, 0:1], None, ALU.mult)
+        nc.vector.tensor_scalar(gq[:], gp[:], -1.0, gain[:, 0:1], ALU.mult, ALU.add)
+
+        def vector_plane():
+            both = [once.tile([P, n], F32, name="both%d" % k) for k in range(2)]
+            for k in range(2):
+                nc.vector.tensor_copy(first[k][:, 0, :], gq[:].indirect(c2_sb[:, entries(k)]))
+            for k in range(2):
+                nc.vector.tensor_tensor(both[k][:], gp[:].indirect(c3_sb[:, entries(k)]), first[k][:, 0, :], ALU.add)
+            for k in range(2):
+                nc.vector.tensor_tensor(second[k][:, 0, :], pre[0][:].indirect(c1_sb[:, entries(k)]), both[k][:], ALU.mult)
+
         picked = {}
+        sources = ((c1_sb, 1.0), (c3_sb, 1.0), (c2_sb, -1.0))
 
         def fetch(items, tag):
-            batch = once.tile([P, len(items), 3, n], F32, name="batch", tag=tag, align_bytes=64)
-            for i, (k, t) in enumerate(items):
-                lc = slice(k * n // 16, (k + 1) * n // 16)
-                nc.scalar.activation(batch[:, i, 0, :], pre[t][:].indirect(c1_sb[:, lc]), ACT.Sigmoid)
-                nc.scalar.activation(batch[:, i, 1, :], pre[t][:].indirect(c3_sb[:, lc]), ACT.Sigmoid)
-                nc.scalar.activation(batch[:, i, 2, :], pre[t][:].indirect(c2_sb[:, lc]), ACT.Sigmoid, scale=-1.0)
-                picked[(k, t)] = (batch, i)
-
-        terms = {}
+            batch = once.tile([P, len(items), n], F32, name="batch", tag=tag, align_bytes=64)
+            for i, (k, t, w) in enumerate(items):
+                places, sign = sources[w]
+                nc.scalar.activation(batch[:, i, :], pre[t][:].indirect(places[:, entries(k)]), ACT.Sigmoid, scale=sign)
+                picked[(k, t, w)] = batch[:, i, :]
 
         def products(k, t):
-            if t == 0:
-                terms[k] = (
-                    work.tile([P, PACK, n], F32, name="na"),
-                    work.tile([P, PACK, n], F32, name="first"),
-                    once.tile([P, PACK, n], F32, name="second", tag="second%d" % (k % 2)),
-                )
-            na, first, second = terms[k]
-            batch, i = picked[(k, t)]
+            na = work.tile([P, n], F32, name="na")
             g = gain[:, t : t + 1]
-            nc.vector.tensor_scalar(na[:, t, :], batch[:, i, 0, :], -1.0, 1.0, ALU.mult, ALU.add)
-            nc.vector.scalar_tensor_tensor(second[:, t, :], batch[:, i, 0, :], g, batch[:, i, 1, :], ALU.mult, ALU.mult)
-            nc.vector.scalar_tensor_tensor(first[:, t, :], na[:, t, :], g, batch[:, i, 2, :], ALU.mult, ALU.mult)
+            a, c, nb = picked[(k, t, 0)], picked[(k, t, 1)], picked[(k, t, 2)]
+            nc.vector.tensor_scalar(na[:], a, -1.0, 1.0, ALU.mult, ALU.add)
+            nc.vector.scalar_tensor_tensor(second[k][:, t, :], a, g, c, ALU.mult, ALU.mult)
+            nc.vector.scalar_tensor_tensor(first[k][:, t, :], na[:], g, nb, ALU.mult, ALU.mult)
 
         def quantise(k):
-            na, first, second = terms[k]
             z = work.tile([P, n, PACK], BF16, name="z", align_bytes=64)
             nc.vector.tensor_tensor(
                 z[:].rearrange("p (c i) t -> p c t i", i=4),
-                first[:].rearrange("p t (c i) -> p c t i", i=4),
-                second[:].rearrange("p t (c i) -> p c t i", i=4),
+                first[k][:].rearrange("p t (c i) -> p c t i", i=4),
+                second[k][:].rearrange("p t (c i) -> p c t i", i=4),
                 ALU.subtract,
             )
-            zw = once.tile([P, n], U32, name="zw", tag="turn%d" % (k % 2), align_bytes=64)
+            zw = once.tile([P, n], U32, name="zw", tag="turn%d" % k, align_bytes=64)
             zs = work.tile([P, n], U8, name="zs", align_bytes=64)
             nc.vector.quantize_mx(zw[:].bitcast(FP8X4), zs[:], z[:].rearrange("p n t -> p (n t)"))
             return zw, zs
 
         def multiply(zw, zs):
-            hacc = psum2.tile([P, PACK, n], F32, name="hacc")
-            for t in range(PACK):
-                cols = slice(P * t, P * (t + 1))
-                nc.tensor.matmul_mx(
-                    hacc[:, t, :], lhsT=w2w_d[:, cols].bitcast(FP8X4), lhsT_scale=w2s_d[:, cols],
-                    rhs=zw[:].bitcast(FP8X4), rhs_scale=zs[:], start=True, stop=True,
-                )
-            return hacc
+            banks = []
+            for pair in range(2):
+                hacc = psum2.tile([P, 2, n], F32, name="hacc%d" % pair)
+                for t in range(2 * pair, 2 * pair + 2):
+                    nc.tensor.matmul_mx(
+                        hacc[:, t % 2, :], lhsT=w2w_d[t].bitcast(FP8X4), lhsT_scale=w2s_d[t],
+                        rhs=zw[:].bitcast(FP8X4), rhs_scale=zs[:], start=True, stop=True,
+                    )
+                banks.append(hacc)
+            return banks
 
-        def put(k, hacc, t0, t1, h):
-            lc = slice(k * n // 16, (k + 1) * n // 16)
-            nc.scalar.copy(h[:, 0 : t1 - t0, :], hacc[:, t0:t1, :])
+        def put(k, banks, t0, t1, h):
+            nc.scalar.copy(h[:, 0 : t1 - t0, :], banks[t0 // 2][:, t0 % 2 : t0 % 2 + t1 - t0, :])
             for t in range(t0, t1):
-                nc.vector.tensor_copy(page[t][:].indirect(slot_sb[:, lc]), h[:, t - t0, :])
+                nc.vector.tensor_copy(page[t][:].indirect(slot_sb[:, entries(k)]), h[:, t - t0, :])
 
-        fetch([(0, 0), (0, 1), (0, 2)], "turn0")
-        fetch([(0, 3), (1, 0), (1, 1), (1, 2)], "turn1")
-        for t in range(PACK - 1):
-            products(0, t)
-        held = None
-        for k in range(nch):
-            products(k, PACK - 1)
-            zw, zs = quantise(k)
-            if k == nch - 1:
-                hb = once.tile([P, PACK, n], F32, name="hb", tag="second%d" % (k % 2))
-                put(k - 1, held, 2, PACK, hb)
-            hacc = multiply(zw, zs)
-            h = work.tile([P, PACK, n], F32, name="h")
-            if k == nch - 2:
-                put(k, hacc, 0, 2, h)
-                held = hacc
-            else:
-                put(k, hacc, 0, PACK, h)
-            if k + 1 < nch:
-                for t in range(PACK - 1):
-                    products(k + 1, t)
-                later = [(k + 1, PACK - 1)]
-                if k + 2 < nch:
-                    later = later + [(k + 2, t) for t in range(PACK - 1)]
-                fetch(later, "turn%d" % (k % 2))
+        order = [(k, t, w) for k in range(2) for t in range(1, PACK) for w in range(3)]
+        for t in range(1, PACK):
+            fetch(order[3 * (t - 1) : 3 * t], "early%d" % t)
+        fetch(order[9 : 9 + AHEAD], "early0")
+        vector_plane()
+        products(0, 1)
+        products(0, 2)
+        products(0, 3)
+        zw, zs = quantise(0)
+        banks0 = multiply(zw, zs)
+        put(0, banks0, 0, 2, once.tile([P, 2, n], F32, name="h00"))
+        put(0, banks0, 2, 3, once.tile([P, 1, n], F32, name="h02"))
+        fetch(order[9 + AHEAD :], "turn0")
+        for t in range(1, PACK):
+            products(1, t)
+        zw, zs = quantise(1)
+        put(0, banks0, 3, 4, once.tile([P, 1, n], F32, name="h03", tag="second1"))
+        banks1 = multiply(zw, zs)
+        put(1, banks1, 0, 2, once.tile([P, 2, n], F32, name="h10"))
+        put(1, banks1, 2, 4, once.tile([P, 2, n], F32, name="h12"))
 
         out_rows = out_0.rearrange("(p t) u -> p t u", t=PACK)
         y = keep.tile([P, PACK, U], BF16, name="y")
+        last = PACK - 1
         for t in range(PACK):
             nc.sync.dma_start(out_rows[:, t, :], page[t][:])
-            if t < PACK - 1:
+            if t < last:
                 nc.scalar.copy(y[:, t, :], page[t][:])
-            else:
-                nc.vector.tensor_copy(y[:, t, :], page[t][:])
+        nc.vector.tensor_copy(y[:, last, 0:SPLIT], page[last][:, 0:SPLIT])
+        nc.scalar.copy(y[:, last, SPLIT:U], page[last][:, SPLIT:U])
+        yi = keep.tile([P, U, PACK], BF16, name="yi", align_bytes=64)
+        dst = yi[:].rearrange("p (c i) t -> p c t i", i=4)
+        src = y[:].rearrange("p t (c i) -> p c t i", i=4)
+        nc.scalar.copy(dst[:, SPLIT // 4 :], src[:, SPLIT // 4 :])
         ow = keep.tile([P, U], I32, name="ow", align_bytes=64)
         osc = keep.tile([P, U], U8, name="osc", align_bytes=64)
         words_out = out_1[0].rearrange("p n t -> p (n t)").bitcast(I32)
-        for half in range(2):
-            cols = slice(half * SPLIT, (half + 1) * SPLIT)
-            yi = keep.tile([P, SPLIT, PACK], BF16, name="yi%d" % half, align_bytes=64)
-            dst = yi[:].rearrange("p (c i) t -> p c t i", i=4)
-            src = y[:, :, cols].rearrange("p t (c i) -> p c t i", i=4)
-            if half == 0:
-                nc.vector.tensor_copy(dst, src)
-            else:
-                nc.vector.tensor_copy(dst[:, 0:32], src[:, 0:32])
-                nc.scalar.copy(dst[:, 32:128], src[:, 32:128])
-            nc.vector.quantize_mx(ow[:, cols].bitcast(FP8X4), osc[:, cols], yi[:].rearrange("p n t -> p (n t)"))
+        half = U // 2
+        nc.vector.tensor_copy(dst[:, 0 : half // 4], src[:, 0 : half // 4])
+        nc.vector.tensor_copy(dst[:, half // 4 : SPLIT // 4], src[:, half // 4 : SPLIT // 4])
+        for c0 in (0, half):
+            cols = slice(c0, c0 + half)
+            nc.vector.quantize_mx(ow[:, cols].bitcast(FP8X4), osc[:, cols], yi[:, cols, :].rearrange("p n t -> p (n t)"))
             nc.sync.dma_start(words_out[:, cols], ow[:, cols])
         for q in range(4):
-            nc.sync.dma_start(out_2[0, 4 * q : 4 * q + 4, :].bitcast(I32), osc[32 * q : 32 * q + 4, :].bitcast(I32))
+            queue = nc.sync if q % 2 == 0 else nc.scalar
+            queue.dma_start(out_2[0, 4 * q : 4 * q + 4, :].bitcast(I32), osc[32 * q : 32 * q + 4, :].bitcast(I32))

@@ -18,7 +18,8 @@ ALU = mybir.AluOpType
 P = 128
 PACK = 4
 CHUNK = 256
-AHEAD = 5
+AHEAD = 3
+ON_SCALAR = ((1, 2), (1, 3))
 SPLIT = 640
 
 
@@ -37,7 +38,6 @@ def tile_picked_noisygate_none_po_kernel(
         work = ctx.enter_context(tc.tile_pool(name="work", bufs=2))
         once = ctx.enter_context(tc.tile_pool(name="once", bufs=1))
         psum = ctx.enter_context(tc.psum_pool(name="psum", bufs=1))
-        psum2 = ctx.enter_context(tc.psum_pool(name="psum2", bufs=2))
 
         offs_sb = lists.tile([P, S // 16], U16, name="offs_sb")
         c1_sb = lists.tile([P, S // 16], U16, name="c1_sb")
@@ -98,38 +98,36 @@ def tile_picked_noisygate_none_po_kernel(
         for t in range(PACK):
             nc.sync.dma_start(page[t][:], mem_rows[:, t, :])
 
-        pre = {}
-        for t in range(PACK):
-            acc = psum.tile([P, S], F32, name="acc%d" % t)
+        pre = {t: keep.tile([P, S], F32, name="pre%d" % t) for t in range(1, PACK)}
+        prob = keep.tile([P, S], F32, name="prob")
+        pieces = [(0, 0, S), (1, 0, S // 2), (1, S // 2, S), (2, 0, S), (3, 0, S)]
+        accs = []
+        for i, (t, j0, j1) in enumerate(pieces):
+            acc = psum.tile([P, S], F32, name="acc", tag="bank%d" % i)
+            accs.append(acc)
             nc.tensor.matmul_mx(
-                acc[:], lhsT=w1w_d[t].bitcast(FP8X4), lhsT_scale=w1s_d[t],
-                rhs=xw_g[:].bitcast(FP8X4), rhs_scale=xs_g[:], start=True, stop=True,
+                acc[:, 0 : j1 - j0], lhsT=w1w_d[t].bitcast(FP8X4), lhsT_scale=w1s_d[t],
+                rhs=xw_g[:, j0:j1].bitcast(FP8X4), rhs_scale=xs_g[:, j0:j1], start=True, stop=True,
             )
-            pre[t] = keep.tile([P, S], F32, name="pre%d" % t)
             if t == 0:
-                nc.scalar.activation(pre[t][:], acc[:], ACT.Sigmoid)
+                nc.scalar.activation(prob[:], acc[:], ACT.Sigmoid)
             else:
-                nc.vector.tensor_copy(pre[t][:], acc[:])
+                nc.vector.tensor_copy(pre[t][:, j0:j1], acc[:, 0 : j1 - j0])
         n = CHUNK
-        first = [once.tile([P, PACK, n], F32, name="first%d" % k) for k in range(2)]
-        second = [once.tile([P, PACK, n], F32, name="second", tag="second%d" % k) for k in range(2)]
+        first = [once.tile([P, PACK, n], F32, name="first", tag="first")]
+        second = [once.tile([P, PACK, n], F32, name="second", tag="second")]
 
         def entries(k):
             return slice(k * n // 16, (k + 1) * n // 16)
 
         gp = keep.tile([P, S], F32, name="gp")
         gq = keep.tile([P, S], F32, name="gq")
-        nc.vector.tensor_scalar(gp[:], pre[0][:], gain[:, 0:1], None, ALU.mult)
+        both = once.tile([P, n], F32, name="both")
+        nc.vector.tensor_scalar(gp[:], prob[:], gain[:, 0:1], None, ALU.mult)
         nc.vector.tensor_scalar(gq[:], gp[:], -1.0, gain[:, 0:1], ALU.mult, ALU.add)
-
-        def vector_plane():
-            both = [once.tile([P, n], F32, name="both%d" % k) for k in range(2)]
-            for k in range(2):
-                nc.vector.tensor_copy(first[k][:, 0, :], gq[:].indirect(c2_sb[:, entries(k)]))
-            for k in range(2):
-                nc.vector.tensor_tensor(both[k][:], gp[:].indirect(c3_sb[:, entries(k)]), first[k][:, 0, :], ALU.add)
-            for k in range(2):
-                nc.vector.tensor_tensor(second[k][:, 0, :], pre[0][:].indirect(c1_sb[:, entries(k)]), both[k][:], ALU.mult)
+        nc.vector.tensor_copy(first[0][:, 0, :], gq[:].indirect(c2_sb[:, entries(0)]))
+        nc.vector.tensor_tensor(both[:], gp[:].indirect(c3_sb[:, entries(0)]), first[0][:, 0, :], ALU.add)
+        nc.vector.tensor_tensor(second[0][:, 0, :], prob[:].indirect(c1_sb[:, entries(0)]), both[:], ALU.mult)
 
         picked = {}
         sources = ((c1_sb, 1.0), (c3_sb, 1.0), (c2_sb, -1.0))
@@ -140,17 +138,23 @@ def tile_picked_noisygate_none_po_kernel(
                 places, sign = sources[w]
                 nc.scalar.activation(batch[:, i, :], pre[t][:].indirect(places[:, entries(k)]), ACT.Sigmoid, scale=sign)
                 picked[(k, t, w)] = batch[:, i, :]
+                if w == 0 and (k, t) in ON_SCALAR:
+                    na = once.tile([P, n], F32, name="na%d%d" % (k, t))
+                    nc.scalar.activation(na[:], batch[:, i, :], ACT.Copy, bias=1.0, scale=-1.0)
+                    picked[(k, t, 3)] = na[:]
 
         def products(k, t):
-            na = work.tile([P, n], F32, name="na")
             g = gain[:, t : t + 1]
             a, c, nb = picked[(k, t, 0)], picked[(k, t, 1)], picked[(k, t, 2)]
-            nc.vector.tensor_scalar(na[:], a, -1.0, 1.0, ALU.mult, ALU.add)
+            if (k, t) not in ON_SCALAR:
+                na = work.tile([P, n], F32, name="na")
+                nc.vector.tensor_scalar(na[:], a, -1.0, 1.0, ALU.mult, ALU.add)
+                picked[(k, t, 3)] = na[:]
             nc.vector.scalar_tensor_tensor(second[k][:, t, :], a, g, c, ALU.mult, ALU.mult)
-            nc.vector.scalar_tensor_tensor(first[k][:, t, :], na[:], g, nb, ALU.mult, ALU.mult)
+            nc.vector.scalar_tensor_tensor(first[k][:, t, :], picked[(k, t, 3)], g, nb, ALU.mult, ALU.mult)
 
         def quantise(k):
-            z = work.tile([P, n, PACK], BF16, name="z", align_bytes=64)
+            z = once.tile([P, n, PACK], BF16, name="z", tag="side%d" % k, align_bytes=64)
             nc.vector.tensor_tensor(
                 z[:].rearrange("p (c i) t -> p c t i", i=4),
                 first[k][:].rearrange("p t (c i) -> p c t i", i=4),
@@ -162,43 +166,47 @@ def tile_picked_noisygate_none_po_kernel(
             nc.vector.quantize_mx(zw[:].bitcast(FP8X4), zs[:], z[:].rearrange("p n t -> p (n t)"))
             return zw, zs
 
-        def multiply(zw, zs):
-            banks = []
-            for pair in range(2):
-                hacc = psum2.tile([P, 2, n], F32, name="hacc%d" % pair)
-                for t in range(2 * pair, 2 * pair + 2):
+        def multiply(zw, zs, groups):
+            sums = {}
+            for bank, t0, t1 in groups:
+                hacc = psum.tile([P, t1 - t0, n], F32, name="hacc", tag="bank%d" % bank)
+                for t in range(t0, t1):
                     nc.tensor.matmul_mx(
-                        hacc[:, t % 2, :], lhsT=w2w_d[t].bitcast(FP8X4), lhsT_scale=w2s_d[t],
+                        hacc[:, t - t0, :], lhsT=w2w_d[t].bitcast(FP8X4), lhsT_scale=w2s_d[t],
                         rhs=zw[:].bitcast(FP8X4), rhs_scale=zs[:], start=True, stop=True,
                     )
-                banks.append(hacc)
-            return banks
+                sums[t0] = (hacc, t1)
+            return sums
 
-        def put(k, banks, t0, t1, h):
-            nc.scalar.copy(h[:, 0 : t1 - t0, :], banks[t0 // 2][:, t0 % 2 : t0 % 2 + t1 - t0, :])
+        def put(k, sums, t0, tag):
+            hacc, t1 = sums[t0]
+            h = once.tile([P, t1 - t0, n], F32, name="h", tag=tag)
+            nc.scalar.copy(h[:], hacc[:])
             for t in range(t0, t1):
                 nc.vector.tensor_copy(page[t][:].indirect(slot_sb[:, entries(k)]), h[:, t - t0, :])
 
-        order = [(k, t, w) for k in range(2) for t in range(1, PACK) for w in range(3)]
+        order = [(1, t, w) for t in (1, 2, 3, 0) for w in range(3)]
         for t in range(1, PACK):
-            fetch(order[3 * (t - 1) : 3 * t], "early%d" % t)
-        fetch(order[9 : 9 + AHEAD], "early0")
-        vector_plane()
-        products(0, 1)
-        products(0, 2)
-        products(0, 3)
+            fetch([(0, t, w) for w in range(3)], "early%d" % t)
+        fetch(order[:AHEAD], "early0")
+        for t in range(1, PACK):
+            products(0, t)
         zw, zs = quantise(0)
-        banks0 = multiply(zw, zs)
-        put(0, banks0, 0, 2, once.tile([P, 2, n], F32, name="h00"))
-        put(0, banks0, 2, 3, once.tile([P, 1, n], F32, name="h02"))
-        fetch(order[9 + AHEAD :], "turn0")
-        for t in range(1, PACK):
+        sums0 = multiply(zw, zs, ((1, 0, 1), (2, 1, 3), (3, 3, 4)))
+        put(0, sums0, 0, "h00")
+        put(0, sums0, 1, "h01")
+        pre[0] = once.tile([P, S], F32, name="pre0", tag="side0", align_bytes=64)
+        nc.scalar.copy(pre[0][:], accs[0][:])
+        fetch(order[AHEAD:], "turn0")
+        first.append(once.tile([P, PACK, n], F32, name="first", tag="first"))
+        second.append(once.tile([P, PACK, n], F32, name="second", tag="second"))
+        for t in (1, 2, 3, 0):
             products(1, t)
         zw, zs = quantise(1)
-        put(0, banks0, 3, 4, once.tile([P, 1, n], F32, name="h03", tag="second1"))
-        banks1 = multiply(zw, zs)
-        put(1, banks1, 0, 2, once.tile([P, 2, n], F32, name="h10"))
-        put(1, banks1, 2, 4, once.tile([P, 2, n], F32, name="h12"))
+        put(0, sums0, 3, "second")
+        sums1 = multiply(zw, zs, ((4, 0, 2), (5, 2, 4)))
+        put(1, sums1, 0, "h10")
+        put(1, sums1, 2, "h12")
 
         out_rows = out_0.rearrange("(p t) u -> p t u", t=PACK)
         y = keep.tile([P, PACK, U], BF16, name="y")
@@ -212,15 +220,16 @@ def tile_picked_noisygate_none_po_kernel(
         yi = keep.tile([P, U, PACK], BF16, name="yi", align_bytes=64)
         dst = yi[:].rearrange("p (c i) t -> p c t i", i=4)
         src = y[:].rearrange("p t (c i) -> p c t i", i=4)
-        nc.scalar.copy(dst[:, SPLIT // 4 :], src[:, SPLIT // 4 :])
+        nc.scalar.copy(dst[:, SPLIT // 4 : 768 // 4], src[:, SPLIT // 4 : 768 // 4])
+        nc.scalar.copy(dst[:, 768 // 4 :], src[:, 768 // 4 :])
         ow = keep.tile([P, U], I32, name="ow", align_bytes=64)
         osc = keep.tile([P, U], U8, name="osc", align_bytes=64)
         words_out = out_1[0].rearrange("p n t -> p (n t)").bitcast(I32)
         half = U // 2
         nc.vector.tensor_copy(dst[:, 0 : half // 4], src[:, 0 : half // 4])
         nc.vector.tensor_copy(dst[:, half // 4 : SPLIT // 4], src[:, half // 4 : SPLIT // 4])
-        for c0 in (0, half):
-            cols = slice(c0, c0 + half)
+        for c0, c1_ in ((0, half), (half, 768), (768, U)):
+            cols = slice(c0, c1_)
             nc.vector.quantize_mx(ow[:, cols].bitcast(FP8X4), osc[:, cols], yi[:, cols, :].rearrange("p n t -> p (n t)"))
             nc.sync.dma_start(words_out[:, cols], ow[:, cols])
         for q in range(4):

@@ -17,15 +17,26 @@ ALU = mybir.AluOpType
 
 P = 128
 PACK = 4
-CHUNK = 256
-AHEAD = 3
-ON_SCALAR = ((1, 2), (1, 3))
+RUN = 4
+CHUNK = S // 2
+AHEAD = 4
+COMPLEMENT_ON_SCALAR = ((1, 2), (1, 3))
 SPLIT = 640
+PIECES = ((0, 512), (512, 768), (768, U))
+A, C, NOT_B, NOT_A = 0, 1, 2, 3
 
 
-def load_scale_rows(queue, plane, rows):
+def load_scale_rows(nc, plane, rows):
     for q in range(4):
-        queue.dma_start(plane[32 * q : 32 * q + 4, :].bitcast(I32), rows[4 * q : 4 * q + 4, :].bitcast(I32))
+        nc.sync.dma_start(plane[32 * q : 32 * q + 4, :].bitcast(I32), rows[4 * q : 4 * q + 4, :].bitcast(I32))
+
+
+def as_words(codes):
+    return codes[0].rearrange("p n t -> p (n t)").bitcast(I32)
+
+
+def entries(chunk):
+    return slice(chunk * CHUNK // 16, (chunk + 1) * CHUNK // 16)
 
 
 def tile_picked_noisygate_none_po_kernel(
@@ -52,26 +63,22 @@ def tile_picked_noisygate_none_po_kernel(
         w2w = keep.tile([P, N], I32, name="w2w", align_bytes=64)
         w2s = keep.tile([P, N], U8, name="w2s", align_bytes=64)
         gain = keep.tile([P, PACK], F32, name="gain")
-        warm = keep.tile([P, 1], F32, name="warm")
-        warm2 = keep.tile([P, 1], F32, name="warm2")
 
         nc.gpsimd.memset(xs[:].bitcast(I32), 0)
         nc.gpsimd.memset(w2s[:].bitcast(I32), 0)
         nc.vector.memset(w1s[:].bitcast(I32), 0)
-        nc.vector.memset(warm[:], 0.0)
-        nc.scalar.activation(warm2[:], warm[:], ACT.Sigmoid)
 
         nc.sync.dma_start(offs_sb[:], offs)
-        nc.sync.dma_start(w1w[:], w1_words[0].rearrange("p n t -> p (n t)").bitcast(I32))
+        nc.sync.dma_start(w1w[:], as_words(w1_words))
         nc.sync.dma_start(c2_sb[:], c2)
-        load_scale_rows(nc.sync, xs, x_scales[0])
-        nc.sync.dma_start(xw[:], x_words[0].rearrange("p n t -> p (n t)").bitcast(I32))
-        load_scale_rows(nc.sync, w1s, w1_scales[0])
+        load_scale_rows(nc, xs, x_scales[0])
+        nc.sync.dma_start(xw[:], as_words(x_words))
+        load_scale_rows(nc, w1s, w1_scales[0])
         nc.sync.dma_start(gain[:], gn.rearrange("(p t) o -> p (t o)", t=PACK))
         nc.sync.dma_start(c1_sb[:], c1)
         nc.sync.dma_start(c3_sb[:], c3)
-        nc.sync.dma_start(w2w[:], w2_words[0].rearrange("p n t -> p (n t)").bitcast(I32))
-        load_scale_rows(nc.sync, w2s, w2_scales[0])
+        nc.sync.dma_start(w2w[:], as_words(w2_words))
+        load_scale_rows(nc, w2s, w2_scales[0])
         nc.sync.dma_start(slot_sb[:], slot)
 
         xs_g = keep.tile([P, S], U8, name="xs_g", align_bytes=64)
@@ -82,8 +89,8 @@ def tile_picked_noisygate_none_po_kernel(
         def deal(raw, dtype, t0, t1, name):
             dealt = keep.tile([P, t1 - t0, P], dtype, name=name, align_bytes=64)
             nc.vector.tensor_copy(
-                dealt[:].rearrange("p t (c i) -> p c t i", i=4),
-                raw[:].rearrange("p (c i t) -> p c t i", i=4, t=PACK)[:, :, t0:t1, :],
+                dealt[:].rearrange("p t (c i) -> p c t i", i=RUN),
+                raw[:].rearrange("p (c i t) -> p c t i", i=RUN, t=PACK)[:, :, t0:t1, :],
             )
             return [dealt[:, t - t0, :] for t in range(t0, t1)]
 
@@ -100,10 +107,10 @@ def tile_picked_noisygate_none_po_kernel(
 
         pre = {t: keep.tile([P, S], F32, name="pre%d" % t) for t in range(1, PACK)}
         prob = keep.tile([P, S], F32, name="prob")
-        pieces = [(0, 0, S), (1, 0, S // 2), (1, S // 2, S), (2, 0, S), (3, 0, S)]
+        parts = [(0, 0, S), (1, 0, S // 2), (1, S // 2, S), (2, 0, S), (3, 0, S)]
         accs = []
-        for i, (t, j0, j1) in enumerate(pieces):
-            acc = psum.tile([P, S], F32, name="acc", tag="bank%d" % i)
+        for bank, (t, j0, j1) in enumerate(parts):
+            acc = psum.tile([P, S], F32, name="acc", tag="bank%d" % bank)
             accs.append(acc)
             nc.tensor.matmul_mx(
                 acc[:, 0 : j1 - j0], lhsT=w1w_d[t].bitcast(FP8X4), lhsT_scale=w1s_d[t],
@@ -113,63 +120,60 @@ def tile_picked_noisygate_none_po_kernel(
                 nc.scalar.activation(prob[:], acc[:], ACT.Sigmoid)
             else:
                 nc.vector.tensor_copy(pre[t][:, j0:j1], acc[:, 0 : j1 - j0])
-        n = CHUNK
-        first = [once.tile([P, PACK, n], F32, name="first", tag="first")]
-        second = [once.tile([P, PACK, n], F32, name="second", tag="second")]
 
-        def entries(k):
-            return slice(k * n // 16, (k + 1) * n // 16)
+        first = [once.tile([P, PACK, CHUNK], F32, name="first", tag="first")]
+        second = [once.tile([P, PACK, CHUNK], F32, name="second", tag="second")]
 
-        gp = keep.tile([P, S], F32, name="gp")
-        gq = keep.tile([P, S], F32, name="gq")
-        both = once.tile([P, n], F32, name="both")
-        nc.vector.tensor_scalar(gp[:], prob[:], gain[:, 0:1], None, ALU.mult)
-        nc.vector.tensor_scalar(gq[:], gp[:], -1.0, gain[:, 0:1], ALU.mult, ALU.add)
-        nc.vector.tensor_copy(first[0][:, 0, :], gq[:].indirect(c2_sb[:, entries(0)]))
-        nc.vector.tensor_tensor(both[:], gp[:].indirect(c3_sb[:, entries(0)]), first[0][:, 0, :], ALU.add)
-        nc.vector.tensor_tensor(second[0][:, 0, :], prob[:].indirect(c1_sb[:, entries(0)]), both[:], ALU.mult)
+        not_b0 = once.tile([P, CHUNK], F32, name="not_b0")
+        both = once.tile([P, CHUNK], F32, name="both")
+        gained = once.tile([P, CHUNK], F32, name="gained")
+        nc.vector.tensor_scalar(not_b0[:], prob[:].indirect(c2_sb[:, entries(0)]), -1.0, 1.0, ALU.mult, ALU.add)
+        nc.vector.tensor_tensor(both[:], prob[:].indirect(c3_sb[:, entries(0)]), not_b0[:], ALU.add)
+        nc.vector.tensor_scalar(first[0][:, 0, :], not_b0[:], gain[:, 0:1], None, ALU.mult)
+        nc.vector.tensor_scalar(gained[:], both[:], gain[:, 0:1], None, ALU.mult)
+        nc.vector.tensor_tensor(second[0][:, 0, :], prob[:].indirect(c1_sb[:, entries(0)]), gained[:], ALU.mult)
 
-        picked = {}
-        sources = ((c1_sb, 1.0), (c3_sb, 1.0), (c2_sb, -1.0))
+        factors = {}
+        sources = {A: (c1_sb, 1.0), C: (c3_sb, 1.0), NOT_B: (c2_sb, -1.0)}
 
         def fetch(items, tag):
-            batch = once.tile([P, len(items), n], F32, name="batch", tag=tag, align_bytes=64)
-            for i, (k, t, w) in enumerate(items):
-                places, sign = sources[w]
-                nc.scalar.activation(batch[:, i, :], pre[t][:].indirect(places[:, entries(k)]), ACT.Sigmoid, scale=sign)
-                picked[(k, t, w)] = batch[:, i, :]
-                if w == 0 and (k, t) in ON_SCALAR:
-                    na = once.tile([P, n], F32, name="na%d%d" % (k, t))
-                    nc.scalar.activation(na[:], batch[:, i, :], ACT.Copy, bias=1.0, scale=-1.0)
-                    picked[(k, t, 3)] = na[:]
+            batch = once.tile([P, len(items), CHUNK], F32, name="batch", tag=tag, align_bytes=64)
+            for i, (chunk, t, factor) in enumerate(items):
+                places, sign = sources[factor]
+                nc.scalar.activation(batch[:, i, :], pre[t][:].indirect(places[:, entries(chunk)]), ACT.Sigmoid, scale=sign)
+                factors[(chunk, t, factor)] = batch[:, i, :]
+                if factor == A and (chunk, t) in COMPLEMENT_ON_SCALAR:
+                    not_a = once.tile([P, CHUNK], F32, name="not_a%d%d" % (chunk, t))
+                    nc.scalar.activation(not_a[:], batch[:, i, :], ACT.Copy, bias=1.0, scale=-1.0)
+                    factors[(chunk, t, NOT_A)] = not_a[:]
 
-        def products(k, t):
+        def products(chunk, t):
             g = gain[:, t : t + 1]
-            a, c, nb = picked[(k, t, 0)], picked[(k, t, 1)], picked[(k, t, 2)]
-            if (k, t) not in ON_SCALAR:
-                na = work.tile([P, n], F32, name="na")
-                nc.vector.tensor_scalar(na[:], a, -1.0, 1.0, ALU.mult, ALU.add)
-                picked[(k, t, 3)] = na[:]
-            nc.vector.scalar_tensor_tensor(second[k][:, t, :], a, g, c, ALU.mult, ALU.mult)
-            nc.vector.scalar_tensor_tensor(first[k][:, t, :], picked[(k, t, 3)], g, nb, ALU.mult, ALU.mult)
+            a, c, not_b = factors[(chunk, t, A)], factors[(chunk, t, C)], factors[(chunk, t, NOT_B)]
+            if (chunk, t) not in COMPLEMENT_ON_SCALAR:
+                not_a = work.tile([P, CHUNK], F32, name="not_a")
+                nc.vector.tensor_scalar(not_a[:], a, -1.0, 1.0, ALU.mult, ALU.add)
+                factors[(chunk, t, NOT_A)] = not_a[:]
+            nc.vector.scalar_tensor_tensor(second[chunk][:, t, :], a, g, c, ALU.mult, ALU.mult)
+            nc.vector.scalar_tensor_tensor(first[chunk][:, t, :], factors[(chunk, t, NOT_A)], g, not_b, ALU.mult, ALU.mult)
 
-        def quantise(k):
-            z = once.tile([P, n, PACK], BF16, name="z", tag="side%d" % k, align_bytes=64)
+        def quantise(chunk):
+            z = once.tile([P, CHUNK, PACK], BF16, name="z", tag="z%d" % chunk, align_bytes=64)
             nc.vector.tensor_tensor(
-                z[:].rearrange("p (c i) t -> p c t i", i=4),
-                first[k][:].rearrange("p t (c i) -> p c t i", i=4),
-                second[k][:].rearrange("p t (c i) -> p c t i", i=4),
+                z[:].rearrange("p (c i) t -> p c t i", i=RUN),
+                first[chunk][:].rearrange("p t (c i) -> p c t i", i=RUN),
+                second[chunk][:].rearrange("p t (c i) -> p c t i", i=RUN),
                 ALU.subtract,
             )
-            zw = once.tile([P, n], U32, name="zw", tag="turn%d" % k, align_bytes=64)
-            zs = work.tile([P, n], U8, name="zs", align_bytes=64)
+            zw = once.tile([P, CHUNK], U32, name="zw", tag="zw%d" % chunk, align_bytes=64)
+            zs = work.tile([P, CHUNK], U8, name="zs", align_bytes=64)
             nc.vector.quantize_mx(zw[:].bitcast(FP8X4), zs[:], z[:].rearrange("p n t -> p (n t)"))
             return zw, zs
 
         def multiply(zw, zs, groups):
             sums = {}
             for bank, t0, t1 in groups:
-                hacc = psum.tile([P, t1 - t0, n], F32, name="hacc", tag="bank%d" % bank)
+                hacc = psum.tile([P, t1 - t0, CHUNK], F32, name="hacc", tag="bank%d" % bank)
                 for t in range(t0, t1):
                     nc.tensor.matmul_mx(
                         hacc[:, t - t0, :], lhsT=w2w_d[t].bitcast(FP8X4), lhsT_scale=w2s_d[t],
@@ -178,28 +182,29 @@ def tile_picked_noisygate_none_po_kernel(
                 sums[t0] = (hacc, t1)
             return sums
 
-        def put(k, sums, t0, tag):
+        def put(chunk, sums, t0, tag):
             hacc, t1 = sums[t0]
-            h = once.tile([P, t1 - t0, n], F32, name="h", tag=tag)
+            h = once.tile([P, t1 - t0, CHUNK], F32, name="h", tag=tag)
             nc.scalar.copy(h[:], hacc[:])
             for t in range(t0, t1):
-                nc.vector.tensor_copy(page[t][:].indirect(slot_sb[:, entries(k)]), h[:, t - t0, :])
+                nc.vector.tensor_copy(page[t][:].indirect(slot_sb[:, entries(chunk)]), h[:, t - t0, :])
 
-        order = [(1, t, w) for t in (1, 2, 3, 0) for w in range(3)]
+        later = [(1, t, factor) for t in (1, 2, 3, 0) for factor in ((C, A, NOT_B) if t == 2 else (A, C, NOT_B))]
         for t in range(1, PACK):
-            fetch([(0, t, w) for w in range(3)], "early%d" % t)
-        fetch(order[:AHEAD], "early0")
+            fetch([(0, t, factor) for factor in (A, C, NOT_B)], "early%d" % t)
+        fetch(later[:AHEAD], "ahead")
         for t in range(1, PACK):
             products(0, t)
         zw, zs = quantise(0)
         sums0 = multiply(zw, zs, ((1, 0, 1), (2, 1, 3), (3, 3, 4)))
         put(0, sums0, 0, "h00")
         put(0, sums0, 1, "h01")
-        pre[0] = once.tile([P, S], F32, name="pre0", tag="side0", align_bytes=64)
+
+        pre[0] = once.tile([P, S], F32, name="pre0", tag="z0", align_bytes=64)
         nc.scalar.copy(pre[0][:], accs[0][:])
-        fetch(order[AHEAD:], "turn0")
-        first.append(once.tile([P, PACK, n], F32, name="first", tag="first"))
-        second.append(once.tile([P, PACK, n], F32, name="second", tag="second"))
+        fetch(later[AHEAD:], "zw0")
+        first.append(once.tile([P, PACK, CHUNK], F32, name="first", tag="first"))
+        second.append(once.tile([P, PACK, CHUNK], F32, name="second", tag="second"))
         for t in (1, 2, 3, 0):
             products(1, t)
         zw, zs = quantise(1)
@@ -209,29 +214,30 @@ def tile_picked_noisygate_none_po_kernel(
         put(1, sums1, 2, "h12")
 
         out_rows = out_0.rearrange("(p t) u -> p t u", t=PACK)
-        y = keep.tile([P, PACK, U], BF16, name="y")
+        rounded = keep.tile([P, PACK, U], BF16, name="rounded")
         last = PACK - 1
         for t in range(PACK):
             nc.sync.dma_start(out_rows[:, t, :], page[t][:])
             if t < last:
-                nc.scalar.copy(y[:, t, :], page[t][:])
-        nc.vector.tensor_copy(y[:, last, 0:SPLIT], page[last][:, 0:SPLIT])
-        nc.scalar.copy(y[:, last, SPLIT:U], page[last][:, SPLIT:U])
-        yi = keep.tile([P, U, PACK], BF16, name="yi", align_bytes=64)
-        dst = yi[:].rearrange("p (c i) t -> p c t i", i=4)
-        src = y[:].rearrange("p t (c i) -> p c t i", i=4)
-        nc.scalar.copy(dst[:, SPLIT // 4 : 768 // 4], src[:, SPLIT // 4 : 768 // 4])
-        nc.scalar.copy(dst[:, 768 // 4 :], src[:, 768 // 4 :])
-        ow = keep.tile([P, U], I32, name="ow", align_bytes=64)
-        osc = keep.tile([P, U], U8, name="osc", align_bytes=64)
-        words_out = out_1[0].rearrange("p n t -> p (n t)").bitcast(I32)
-        half = U // 2
-        nc.vector.tensor_copy(dst[:, 0 : half // 4], src[:, 0 : half // 4])
-        nc.vector.tensor_copy(dst[:, half // 4 : SPLIT // 4], src[:, half // 4 : SPLIT // 4])
-        for c0, c1_ in ((0, half), (half, 768), (768, U)):
-            cols = slice(c0, c1_)
-            nc.vector.quantize_mx(ow[:, cols].bitcast(FP8X4), osc[:, cols], yi[:, cols, :].rearrange("p n t -> p (n t)"))
-            nc.sync.dma_start(words_out[:, cols], ow[:, cols])
+                nc.scalar.copy(rounded[:, t, :], page[t][:])
+        nc.vector.tensor_copy(rounded[:, last, 0:SPLIT], page[last][:, 0:SPLIT])
+        nc.scalar.copy(rounded[:, last, SPLIT:U], page[last][:, SPLIT:U])
+
+        woven = keep.tile([P, U, PACK], BF16, name="woven", align_bytes=64)
+        dst = woven[:].rearrange("p (c i) t -> p c t i", i=RUN)
+        src = rounded[:].rearrange("p t (c i) -> p c t i", i=RUN)
+        second_piece, third_piece = PIECES[1][0], PIECES[2][0]
+        for u0, u1 in ((SPLIT, third_piece), (third_piece, U)):
+            nc.scalar.copy(dst[:, u0 // RUN : u1 // RUN], src[:, u0 // RUN : u1 // RUN])
+        out_words = keep.tile([P, U], I32, name="out_words", align_bytes=64)
+        out_scales = keep.tile([P, U], U8, name="out_scales", align_bytes=64)
+        for u0, u1 in ((0, second_piece), (second_piece, SPLIT)):
+            nc.vector.tensor_copy(dst[:, u0 // RUN : u1 // RUN], src[:, u0 // RUN : u1 // RUN])
+        for u0, u1 in PIECES:
+            nc.vector.quantize_mx(
+                out_words[:, u0:u1].bitcast(FP8X4), out_scales[:, u0:u1], woven[:, u0:u1, :].rearrange("p n t -> p (n t)")
+            )
+            nc.sync.dma_start(as_words(out_1)[:, u0:u1], out_words[:, u0:u1])
         for q in range(4):
             queue = nc.sync if q % 2 == 0 else nc.scalar
-            queue.dma_start(out_2[0, 4 * q : 4 * q + 4, :].bitcast(I32), osc[32 * q : 32 * q + 4, :].bitcast(I32))
+            queue.dma_start(out_2[0, 4 * q : 4 * q + 4, :].bitcast(I32), out_scales[32 * q : 32 * q + 4, :].bitcast(I32))

from contextlib import ExitStack

import concourse.mybir as mybir

K, T, S, N, H, U = 512, 2048, 512, 512, 512, 1024
FLOPS = 2 * K * H * S + 2 * H * N * S

F32 = mybir.dt.float32
BF16 = mybir.dt.bfloat16
I32 = mybir.dt.int32
U32 = mybir.dt.uint32
U16 = mybir.dt.uint16
U8 = mybir.dt.uint8
FP8X4 = mybir.dt.float8_e4m3fn_x4
ACT = mybir.ActivationFunctionType
ALU = mybir.AluOpType

P = 128
PACK = 4
RUN = 4
CHUNK = S // 2
AHEAD = 4
COMPLEMENT_ON_SCALAR = ((1, 2), (1, 3))
SPLIT = 640
PIECES = ((0, 512), (512, 768), (768, U))
A, C, NOT_B, NOT_A = 0, 1, 2, 3


def load_scale_rows(nc, plane, rows):
    for q in range(4):
        nc.sync.dma_start(plane[32 * q : 32 * q + 4, :].bitcast(I32), rows[4 * q : 4 * q + 4, :].bitcast(I32))


def as_words(codes):
    return codes[0].rearrange("p n t -> p (n t)").bitcast(I32)


def entries(chunk):
    return slice(chunk * CHUNK // 16, (chunk + 1) * CHUNK // 16)


def tile_picked_noisygate_none_po_kernel(
    tc, x_words, x_scales, w1_words, w1_scales, gn, w2_words, w2_scales, mem, offs, c1, c2, c3, slot, out_0, out_1, out_2
):
    nc = tc.nc
    with ExitStack() as ctx:
        lists = ctx.enter_context(tc.tile_pool(name="lists", bufs=1))
        keep = ctx.enter_context(tc.tile_pool(name="keep", bufs=1))
        work = ctx.enter_context(tc.tile_pool(name="work", bufs=2))
        once = ctx.enter_context(tc.tile_pool(name="once", bufs=1))
        psum = ctx.enter_context(tc.psum_pool(name="psum", bufs=1))

        offs_sb = lists.tile([P, S // 16], U16, name="offs_sb")
        c1_sb = lists.tile([P, S // 16], U16, name="c1_sb")
        c2_sb = lists.tile([P, S // 16], U16, name="c2_sb")
        c3_sb = lists.tile([P, S // 16], U16, name="c3_sb")
        slot_sb = lists.tile([P, S // 16], U16, name="slot_sb")

        xs = keep.tile([P, T], U8, name="xs", tag="reuse1", align_bytes=64)
        xw = keep.tile([P, T], I32, name="xw", tag="reuse0", align_bytes=64)
        w1w = keep.tile([P, H], I32, name="w1w", tag="reuse2", align_bytes=64)
        w1s = keep.tile([P, H], U8, name="w1s", tag="reuse3", align_bytes=64)
        w2w = keep.tile([P, N], I32, name="w2w", align_bytes=64)
        w2s = keep.tile([P, N], U8, name="w2s", align_bytes=64)
        gain = keep.tile([P, PACK], F32, name="gain")

        nc.gpsimd.memset(xs[:].bitcast(I32), 0)
        nc.gpsimd.memset(w2s[:].bitcast(I32), 0)
        nc.vector.memset(w1s[:].bitcast(I32), 0)

        nc.sync.dma_start(offs_sb[:], offs)
        nc.sync.dma_start(w1w[:], as_words(w1_words))
        nc.sync.dma_start(c2_sb[:], c2)
        load_scale_rows(nc, xs, x_scales[0])
        nc.sync.dma_start(xw[:], as_words(x_words))
        load_scale_rows(nc, w1s, w1_scales[0])
        nc.sync.dma_start(gain[:], gn.rearrange("(p t) o -> p (t o)", t=PACK))
        nc.sync.dma_start(c1_sb[:], c1)
        nc.sync.dma_start(c3_sb[:], c3)
        nc.sync.dma_start(w2w[:], as_words(w2_words))
        load_scale_rows(nc, w2s, w2_scales[0])
        nc.sync.dma_start(slot_sb[:], slot)

        xs_g = keep.tile([P, S], U8, name="xs_g", align_bytes=64)
        xw_g = keep.tile([P, S], U32, name="xw_g", align_bytes=64)
        nc.vector.tensor_copy(xs_g[:], xs[:].indirect(offs_sb[:]))
        nc.vector.tensor_copy(xw_g[:], xw[:].bitcast(U32).indirect(offs_sb[:]))

        def deal(raw, dtype, t0, t1, name):
            dealt = keep.tile([P, t1 - t0, P], dtype, name=name, align_bytes=64)
            nc.vector.tensor_copy(
                dealt[:].rearrange("p t (c i) -> p c t i", i=RUN),
                raw[:].rearrange("p (c i t) -> p c t i", i=RUN, t=PACK)[:, :, t0:t1, :],
            )
            return [dealt[:, t - t0, :] for t in range(t0, t1)]

        w1w_d = deal(w1w, I32, 0, PACK, "w1w_d")
        w1s_d = deal(w1s, U8, 0, 1, "w1s_head")
        w1s_d = w1s_d + deal(w1s, U8, 1, PACK, "w1s_rest")
        w2w_d = deal(w2w, I32, 0, PACK, "w2w_d")
        w2s_d = deal(w2s, U8, 0, PACK, "w2s_d")

        page = [keep.tile([P, U], F32, name="page%d" % t, tag="reuse%d" % t, align_bytes=64) for t in range(PACK)]
        mem_rows = mem.rearrange("(p t) u -> p t u", t=PACK)
        for t in range(PACK):
            nc.sync.dma_start(page[t][:], mem_rows[:, t, :])

        pre = {t: keep.tile([P, S], F32, name="pre%d" % t) for t in range(1, PACK)}
        prob = keep.tile([P, S], F32, name="prob")
        parts = [(0, 0, S), (1, 0, S // 2), (1, S // 2, S), (2, 0, S), (3, 0, S)]
        accs = []
        for bank, (t, j0, j1) in enumerate(parts):
            acc = psum.tile([P, S], F32, name="acc", tag="bank%d" % bank)
            accs.append(acc)
            nc.tensor.matmul_mx(
                acc[:, 0 : j1 - j0], lhsT=w1w_d[t].bitcast(FP8X4), lhsT_scale=w1s_d[t],
                rhs=xw_g[:, j0:j1].bitcast(FP8X4), rhs_scale=xs_g[:, j0:j1], start=True, stop=True,
            )
            if t == 0:
                nc.scalar.activation(prob[:], acc[:], ACT.Sigmoid)
            else:
                nc.vector.tensor_copy(pre[t][:, j0:j1], acc[:, 0 : j1 - j0])

        first = [once.tile([P, PACK, CHUNK], F32, name="first", tag="first")]
        second = [once.tile([P, PACK, CHUNK], F32, name="second", tag="second")]

        not_b0 = once.tile([P, CHUNK], F32, name="not_b0")
        both = once.tile([P, CHUNK], F32, name="both")
        gained = once.tile([P, CHUNK], F32, name="gained")
        nc.vector.tensor_scalar(not_b0[:], prob[:].indirect(c2_sb[:, entries(0)]), -1.0, 1.0, ALU.mult, ALU.add)
        nc.vector.tensor_tensor(both[:], prob[:].indirect(c3_sb[:, entries(0)]), not_b0[:], ALU.add)
        nc.vector.tensor_scalar(first[0][:, 0, :], not_b0[:], gain[:, 0:1], None, ALU.mult)
        nc.vector.tensor_scalar(gained[:], both[:], gain[:, 0:1], None, ALU.mult)
        nc.vector.tensor_tensor(second[0][:, 0, :], prob[:].indirect(c1_sb[:, entries(0)]), gained[:], ALU.mult)

        factors = {}
        sources = {A: (c1_sb, 1.0), C: (c3_sb, 1.0), NOT_B: (c2_sb, -1.0)}

        def fetch(items, tag):
            batch = once.tile([P, len(items), CHUNK], F32, name="batch", tag=tag, align_bytes=64)
            for i, (chunk, t, factor) in enumerate(items):
                places, sign = sources[factor]
                nc.scalar.activation(batch[:, i, :], pre[t][:].indirect(places[:, entries(chunk)]), ACT.Sigmoid, scale=sign)
                factors[(chunk, t, factor)] = batch[:, i, :]
                if factor == A and (chunk, t) in COMPLEMENT_ON_SCALAR:
                    not_a = once.tile([P, CHUNK], F32, name="not_a%d%d" % (chunk, t))
                    nc.scalar.activation(not_a[:], batch[:, i, :], ACT.Copy, bias=1.0, scale=-1.0)
                    factors[(chunk, t, NOT_A)] = not_a[:]

        def products(chunk, t):
            g = gain[:, t : t + 1]
            a, c, not_b = factors[(chunk, t, A)], factors[(chunk, t, C)], factors[(chunk, t, NOT_B)]
            if (chunk, t) not in COMPLEMENT_ON_SCALAR:
                not_a = work.tile([P, CHUNK], F32, name="not_a")
                nc.vector.tensor_scalar(not_a[:], a, -1.0, 1.0, ALU.mult, ALU.add)
                factors[(chunk, t, NOT_A)] = not_a[:]
            nc.vector.scalar_tensor_tensor(second[chunk][:, t, :], a, g, c, ALU.mult, ALU.mult)
            nc.vector.scalar_tensor_tensor(first[chunk][:, t, :], factors[(chunk, t, NOT_A)], g, not_b, ALU.mult, ALU.mult)

        def quantise(chunk):
            z = once.tile([P, CHUNK, PACK], BF16, name="z", tag="z%d" % chunk, align_bytes=64)
            nc.vector.tensor_tensor(
                z[:].rearrange("p (c i) t -> p c t i", i=RUN),
                first[chunk][:].rearrange("p t (c i) -> p c t i", i=RUN),
                second[chunk][:].rearrange("p t (c i) -> p c t i", i=RUN),
                ALU.subtract,
            )
            zw = once.tile([P, CHUNK], U32, name="zw", tag="zw%d" % chunk, align_bytes=64)
            zs = work.tile([P, CHUNK], U8, name="zs", align_bytes=64)
            nc.vector.quantize_mx(zw[:].bitcast(FP8X4), zs[:], z[:].rearrange("p n t -> p (n t)"))
            return zw, zs

        def multiply(zw, zs, groups):
            sums = {}
            for bank, t0, t1 in groups:
                hacc = psum.tile([P, t1 - t0, CHUNK], F32, name="hacc", tag="bank%d" % bank)
                for t in range(t0, t1):
                    nc.tensor.matmul_mx(
                        hacc[:, t - t0, :], lhsT=w2w_d[t].bitcast(FP8X4), lhsT_scale=w2s_d[t],
                        rhs=zw[:].bitcast(FP8X4), rhs_scale=zs[:], start=True, stop=True,
                    )
                sums[t0] = (hacc, t1)
            return sums

        def put(chunk, sums, t0, tag):
            hacc, t1 = sums[t0]
            h = once.tile([P, t1 - t0, CHUNK], F32, name="h", tag=tag)
            nc.scalar.copy(h[:], hacc[:])
            for t in range(t0, t1):
                nc.vector.tensor_copy(page[t][:].indirect(slot_sb[:, entries(chunk)]), h[:, t - t0, :])

        later = [(1, t, factor) for t in (1, 2, 3, 0) for factor in ((C, A, NOT_B) if t == 2 else (A, C, NOT_B))]
        for t in range(1, PACK):
            fetch([(0, t, factor) for factor in (A, C, NOT_B)], "early%d" % t)
        fetch(later[:AHEAD], "ahead")
        for t in range(1, PACK):
            products(0, t)
        zw, zs = quantise(0)
        sums0 = multiply(zw, zs, ((1, 0, 1), (2, 1, 3), (3, 3, 4)))
        put(0, sums0, 0, "h00")
        put(0, sums0, 1, "h01")

        pre[0] = once.tile([P, S], F32, name="pre0", tag="z0", align_bytes=64)
        nc.scalar.copy(pre[0][:], accs[0][:])
        fetch(later[AHEAD:], "zw0")
        first.append(once.tile([P, PACK, CHUNK], F32, name="first", tag="first"))
        second.append(once.tile([P, PACK, CHUNK], F32, name="second", tag="second"))
        for t in (1, 2, 3, 0):
            products(1, t)
        zw, zs = quantise(1)
        put(0, sums0, 3, "second")
        sums1 = multiply(zw, zs, ((4, 0, 2), (5, 2, 4)))
        put(1, sums1, 0, "h10")
        put(1, sums1, 2, "h12")

        out_rows = out_0.rearrange("(p t) u -> p t u", t=PACK)
        rounded = keep.tile([P, PACK, U], BF16, name="rounded")
        last = PACK - 1
        for t in range(PACK):
            nc.sync.dma_start(out_rows[:, t, :], page[t][:])
            if t < last:
                nc.scalar.copy(rounded[:, t, :], page[t][:])
        nc.vector.tensor_copy(rounded[:, last, 0:SPLIT], page[last][:, 0:SPLIT])
        nc.scalar.copy(rounded[:, last, SPLIT:U], page[last][:, SPLIT:U])

        woven = keep.tile([P, U, PACK], BF16, name="woven", align_bytes=64)
        dst = woven[:].rearrange("p (c i) t -> p c t i", i=RUN)
        src = rounded[:].rearrange("p t (c i) -> p c t i", i=RUN)
        second_piece, third_piece = PIECES[1][0], PIECES[2][0]
        for u0, u1 in ((SPLIT, third_piece), (third_piece, U)):
            nc.scalar.copy(dst[:, u0 // RUN : u1 // RUN], src[:, u0 // RUN : u1 // RUN])
        out_words = keep.tile([P, U], I32, name="out_words", align_bytes=64)
        out_scales = keep.tile([P, U], U8, name="out_scales", align_bytes=64)
        for u0, u1 in ((0, second_piece), (second_piece, SPLIT)):
            nc.vector.tensor_copy(dst[:, u0 // RUN : u1 // RUN], src[:, u0 // RUN : u1 // RUN])
        for u0, u1 in PIECES:
            nc.vector.quantize_mx(
                out_words[:, u0:u1].bitcast(FP8X4), out_scales[:, u0:u1], woven[:, u0:u1, :].rearrange("p n t -> p (n t)")
            )
            nc.sync.dma_start(as_words(out_1)[:, u0:u1], out_words[:, u0:u1])
        for q in range(4):
            queue = nc.sync if q % 2 == 0 else nc.scalar
            queue.dma_start(out_2[0, 4 * q : 4 * q + 4, :].bitcast(I32), out_scales[32 * q : 32 * q + 4, :].bitcast(I32))
